import numpy as np
import ml_dtypes


def mxq(x, axis, fmt="e4m3"):
    dtype, down = {"e4m3": (ml_dtypes.float8_e4m3fn, 7), "e5m2": (ml_dtypes.float8_e5m2, 14)}[fmt]
    v = np.moveaxis(np.asarray(x, np.float32).astype(ml_dtypes.bfloat16).astype(np.float64), axis, -1)
    blocks = v.reshape(v.shape[:-1] + (-1, 32))
    amax = np.abs(blocks).max(-1, keepdims=True)
    byte = np.maximum(np.where(amax > 0, np.frexp(amax)[1] - 1 + 127, 0) - down, 1)
    scale = np.exp2(byte - 127.0)
    codes = (blocks / scale).astype(np.float32).astype(dtype).astype(np.float64)
    return np.moveaxis((codes * scale).reshape(v.shape), -1, axis)


WIDE = False


def mx_kscale(k):
    if not WIDE:
        return np.ones(k)
    levels = np.array([10, -10, 5, -5, 0])
    if k % 512:
        return np.exp2(np.random.permutation(np.resize(levels, k // 32))).repeat(32)
    a = np.empty((k // 512, 16))
    for p in range(k // 512):
        a[p, :8] = np.random.permutation(np.resize(levels, 8))
        for g in range(8):
            far = levels[np.abs(levels - a[p, g]) >= 10]
            a[p, g + 8] = far[np.random.randint(len(far))]
    return np.exp2(a.ravel()).repeat(32)


def f64(x):
    return np.asarray(x).astype(np.float64)


def striped(idx):
    return np.tile(idx.reshape(-1, 16).T, (8, 1)).astype(np.uint16)


def unstriped(offs):
    return offs[:16].T.reshape(-1).astype(np.int64)


E2M1 = np.array([0.0, 0.5, 1.0, 1.5, 2.0, 3.0, 4.0, 6.0, -0.0, -0.5, -1.0, -1.5, -2.0, -3.0, -4.0, -6.0])


def pack_weight(w, fmt):
    k, n = w.shape
    w = f64(np.asarray(w, np.float32).astype(ml_dtypes.bfloat16)).reshape(k // 32, 32, n)
    amax = np.abs(w).max(1)
    if fmt == "e4m3":
        byte = np.frexp(amax)[1] - 1 + 127 - 7
    else:
        mant, ex = np.frexp(amax / 6.0)
        byte = np.where(mant > 0.5, ex, ex - 1) + 127
    byte = np.clip(np.where(amax > 0, byte, 1), 1, 254)
    scaled = (w * np.exp2(127.0 - byte)[:, None, :]).reshape(k, n).astype(np.float32)
    by_word = np.ascontiguousarray(scaled.reshape(k // 512, 128, 4, n).transpose(0, 1, 3, 2))
    if fmt == "e4m3":
        words = by_word.astype(ml_dtypes.float8_e4m3fn).view(np.uint8)
    else:
        c = by_word.astype(ml_dtypes.float4_e2m1fn).view(np.uint8) & 0xF
        words = (c[..., 0::2] | (c[..., 1::2] << 4)).reshape(k // 512, 128, 2 * n)
    return np.ascontiguousarray(words), np.ascontiguousarray(byte.astype(np.uint8).reshape(k // 512, 16, n))


def unpack_weight(words, scales, fmt):
    g, _, n = scales.shape
    words = np.ascontiguousarray(words).reshape(g, 128, n, -1)
    if fmt == "e4m3":
        vals = words.view(ml_dtypes.float8_e4m3fn).astype(np.float64)
    else:
        nib = np.empty((g, 128, n, 4), np.uint8)
        nib[..., 0::2] = words & 0xF
        nib[..., 1::2] = words >> 4
        vals = E2M1[nib]
    vals = vals * np.repeat(np.exp2(scales.astype(np.float64) - 127.0), 8, axis=1)[..., None]
    return vals.transpose(0, 1, 3, 2).reshape(g * 512, n)


def gelu(v):
    return 0.5 * v * (1.0 + np.tanh(np.sqrt(2.0 / np.pi) * (v + 0.044715 * v**3)))


def striped8(idx):
    return np.concatenate([v.reshape(-1, 16).T for v in idx]).astype(np.uint16)


def unstriped8(offs):
    return np.stack([offs[16 * g:16 * g + 16].T.reshape(-1) for g in range(8)]).astype(np.int64)


def runs(v, idx8):
    k = np.arange(v.shape[0])
    return v[k[:, None], idx8[k % 512 // 64]]


K, T, S, H, P, M, N = 1024, 2048, 1024, 1024, 512, 1024, 384

def setup_inputs():
    n = np.random.standard_normal
    s = mx_kscale(K)[:, None]
    u = mx_kscale(H)[:, None]
    u2 = mx_kscale(M)[:, None]
    tab_words, tab_scales = pack_weight(n((K, T)) * s, "e4m3")
    w1_words, w1_scales = pack_weight(0.95 * n((K, H)) / np.sqrt(K) / s, "e2m1")
    w4_words, w4_scales = pack_weight(n((H, N)) / np.sqrt(H) / u, "e4m3")
    return {
        "tab_words": tab_words, "tab_scales": tab_scales,
        "offs": striped(np.random.permutation(T)[:S]),
        "w1_words": w1_words, "w1_scales": w1_scales,
        "offs2": striped8(np.stack([np.random.permutation(S)[:P] for _ in range(8)])),
        "thr": np.repeat(n(H // 64), 64).astype(np.float32),
        "pat": (1.6 * n((H, P)) * u).astype(np.float32),
        "w2": (1.6 * n((H, M)) / np.sqrt(H) / u).astype(np.float32),
        "b2": (0.5 * n(M)).astype(np.float32),
        "gain": (np.random.uniform(0.5, 2.0, M) * u2[:, 0]).astype(np.float32),
        "w3": (n((M, N)) / np.sqrt(M) / u2).astype(np.float32),
        "w4_words": w4_words, "w4_scales": w4_scales,
    }

def reference(tab_words, tab_scales, offs, w1_words, w1_scales, offs2, thr, pat, w2, b2, gain, w3, w4_words, w4_scales):
    v = unpack_weight(tab_words, tab_scales, "e4m3")[:, unstriped(offs)]
    w1 = unpack_weight(w1_words, w1_scales, "e2m1")
    w4 = unpack_weight(w4_words, w4_scales, "e4m3")
    h = w1.T @ v
    hp = runs(h, unstriped8(offs2))
    a = 1.0 / (1.0 + np.exp(-(hp + f64(thr)[:, None])))
    y = a * f64(pat)
    yq = mxq(y, 0, "e4m3")
    d = (mxq(f64(w2), 0, "e4m3").T @ yq) + f64(b2)[:, None]
    act = 0.5 * d * (1.0 + np.tanh(0.7978845608028654 * (d + 0.044715 * d * d * d)))
    f = act * f64(gain)[:, None]
    fq = mxq(f, 0, "e4m3")
    return mxq(f64(w3), 0, "e4m3").T @ fq + w4.T @ yq

@@ -1,0 +1,331 @@
+from contextlib import ExitStack
+
+import concourse.mybir as mybir
+
+K, T, S, H, PICKS, M, N = 1024, 2048, 1024, 1024, 512, 1024, 384
+FLOPS = 2 * (K * H * S + H * M * PICKS + M * N * PICKS + H * N * PICKS)
+
+F32 = mybir.dt.float32
+BF16 = mybir.dt.bfloat16
+I32 = mybir.dt.int32
+U32 = mybir.dt.uint32
+U16 = mybir.dt.uint16
+U8 = mybir.dt.uint8
+FP8X4 = mybir.dt.float8_e4m3fn_x4
+FP4X4 = mybir.dt.float4_e2m1fn_x4
+ACT = mybir.ActivationFunctionType
+MULT = mybir.AluOpType.mult
+
+P = 128
+PACK = 4
+K_PASS = P * PACK
+PASSES = 2
+BANK = 512
+HALF = PICKS // 2
+N_TILES = N // P
+
+
+def tile_list_fence_section_gates_kernel(
+    tc, tab_words, tab_scales, offs, w1_words, w1_scales, offs2, thr, pat, w2, b2, gain, w3, w4_words, w4_scales, out
+):
+    nc = tc.nc
+    two = range(2)
+    four = range(PACK)
+    with ExitStack() as ctx:
+        lists = ctx.enter_context(tc.tile_pool(name="lists", bufs=1))
+        keep = ctx.enter_context(tc.tile_pool(name="keep", bufs=1))
+        psum = ctx.enter_context(tc.psum_pool(name="psum", bufs=8))
+
+        def sb(name, shape, dtype, tag="", bufs=1):
+            return keep.tile(shape, dtype, name=name, tag=tag or name, bufs=bufs, align_bytes=64)
+
+        offs_sb = lists.tile([P, S // 16], U16, name="offs_sb")
+        offs2_sb = lists.tile([P, PICKS // 16], U16, name="offs2_sb")
+
+        tab_scale_sb = sb("tab_scale_sb", [P, T], U8)
+        w1_scale_raw = sb("w1_scale_raw", [P, PASSES, H], U8)
+        picked_scale = sb("picked_scale", [P, S], U8)
+        picked_planes = sb("picked_planes", [P, PASSES, S], U8)
+        w4_scale_sb = sb("w4_scale_sb", [P, PASSES, N], U8)
+        nc.vector.memset(tab_scale_sb[32:64, :].bitcast(I32), 0)
+        nc.vector.memset(tab_scale_sb[64:128, :].bitcast(I32), 0)
+        nc.gpsimd.memset(w1_scale_raw[:].bitcast(I32), 0)
+        nc.gpsimd.memset(picked_planes[:].bitcast(I32), 0)
+        nc.gpsimd.memset(w4_scale_sb[:].bitcast(I32), 0)
+
+        nc.sync.dma_start(offs_sb[:], offs)
+        nc.sync.dma_start(tab_scale_sb[0:32, :].bitcast(I32), tab_scales.rearrange("a r n -> r a n").bitcast(I32))
+        tab_sb = [sb("tab_sb%d" % a, [P, T], U32) for a in two]
+        w1_raw = [sb("w1_raw%d" % b, [P, PASSES, K_PASS], U16) for b in two]
+
+        def load_tab(a):
+            nc.sync.dma_start(tab_sb[a][:].bitcast(I32), tab_words[a].rearrange("p n t -> p (n t)").bitcast(I32))
+
+        def load_w1(b):
+            cols = w1_words[:, :, 2 * b * K_PASS : 2 * (b + 1) * K_PASS]
+            nc.sync.dma_start(w1_raw[b][:].bitcast(I32), cols.rearrange("a p n -> p a n").bitcast(I32))
+
+        load_tab(0)
+        for q in four:
+            nc.sync.dma_start(
+                w1_scale_raw[32 * q : 32 * q + 4].bitcast(I32),
+                w1_scales[:, 4 * q : 4 * q + 4, :].rearrange("a r n -> r a n").bitcast(I32),
+            )
+        load_w1(0)
+        load_tab(1)
+        load_w1(1)
+        nc.sync.dma_start(offs2_sb[:], offs2)
+        thr_sb = sb("thr_sb", [P, PASSES, PACK], F32)
+        nc.sync.dma_start(thr_sb[:], thr.rearrange("(b p t) -> p b t", p=P, t=PACK))
+
+        w2_raw = {}
+        pat_sb = {}
+
+        def load_w2(a, b):
+            w2_raw[a, b] = sb("w2_raw%d%d" % (a, b), [P, PACK, K_PASS], F32)
+            rows = w2[a * K_PASS : (a + 1) * K_PASS, b * K_PASS : (b + 1) * K_PASS]
+            nc.sync.dma_start(w2_raw[a, b][:], rows.rearrange("(p j) c -> p j c", j=PACK))
+
+        def load_pat(b, half):
+            pat_sb[b, half] = sb("pat_sb%d%d" % (b, half), [P, PACK, HALF], F32)
+            rows = pat[b * K_PASS : (b + 1) * K_PASS, half * HALF : (half + 1) * HALF]
+            nc.sync.dma_start(pat_sb[b, half][:], rows.rearrange("(p j) c -> p j c", j=PACK))
+
+        load_w2(0, 0)
+        load_w2(1, 0)
+        load_pat(0, 0)
+        load_pat(1, 0)
+        load_w2(0, 1)
+        load_w2(1, 1)
+        load_pat(0, 1)
+        load_pat(1, 1)
+        b2_sb = sb("b2_sb", [P, PASSES, PACK], F32)
+        nc.sync.dma_start(b2_sb[:], b2.rearrange("(b p t) -> p b t", p=P, t=PACK))
+        gain_sb = sb("gain_sb", [P, PASSES, PACK], F32)
+        nc.sync.dma_start(gain_sb[:], gain.rearrange("(b p t) -> p b t", p=P, t=PACK))
+        w3_raw = [sb("w3_raw%d" % a, [P, PACK, N], F32) for a in two]
+        for a in two:
+            nc.sync.dma_start(w3_raw[a][:], w3[a * K_PASS : (a + 1) * K_PASS, :].rearrange("(p j) c -> p j c", j=PACK))
+        for q in four:
+            nc.sync.dma_start(
+                w4_scale_sb[32 * q : 32 * q + 4].bitcast(I32),
+                w4_scales[:, 4 * q : 4 * q + 4, :].rearrange("a r n -> r a n").bitcast(I32),
+            )
+        w4_sb = sb("w4_sb", [P, PASSES, N], U32)
+        nc.sync.dma_start(w4_sb[:].bitcast(I32), w4_words.rearrange("a p n t -> p a (n t)").bitcast(I32))
+
+        nc.vector.tensor_copy(picked_scale[:], tab_scale_sb[:].indirect(offs_sb[:]))
+        for q in four:
+            nc.scalar.dma_start(
+                picked_planes[32 * q : 32 * q + 4].bitcast(I32),
+                picked_scale[8 * q : 8 * q + 8, :].bitcast(I32),
+            )
+        picked = {}
+
+        def pick_words(a, s):
+            picked[a, s] = sb("picked%d%d" % (a, s), [P, BANK], U32)
+            nc.vector.tensor_copy(picked[a, s][:], tab_sb[a][:].indirect(offs_sb[:, 32 * s : 32 * s + 32]))
+
+        w1_sb = [sb("w1_sb%d" % b, [P, PASSES, K_PASS], U16) for b in two]
+        w1_scale_sb = [sb("w1_scale_sb%d" % b, [P, PASSES, K_PASS], U8) for b in two]
+
+        def deal_w1_words(b):
+            nc.scalar.copy(
+                w1_sb[b][:].rearrange("p a (t m) -> p a t m", t=PACK),
+                w1_raw[b][:].rearrange("p a (m t) -> p a t m", t=PACK),
+            )
+
+        def deal_w1_scales(b):
+            nc.vector.tensor_copy(
+                w1_scale_sb[b][:].rearrange("p a (t m) -> p a t m", t=PACK),
+                w1_scale_raw[:, :, b * K_PASS : (b + 1) * K_PASS].rearrange("p a (m t) -> p a t m", t=PACK),
+            )
+
+        pick_words(0, 0)
+        pick_words(0, 1)
+        deal_w1_words(0)
+        deal_w1_scales(0)
+        pick_words(1, 0)
+        pick_words(1, 1)
+        deal_w1_words(1)
+        deal_w1_scales(1)
+
+        def quantize(name, grouped, width):
+            codes = sb(name + "_codes", [P, width], U32)
+            scales = sb(name + "_scales", [P, width], U8)
+            nc.vector.quantize_mx(
+                out=codes[:].bitcast(FP8X4), scales=scales[:], in_=grouped[:].rearrange("p c j -> p (c j)")
+            )
+            return codes, scales
+
+        w2_bf = {}
+        w2_q = {}
+
+        def round_w2(a, b, copy):
+            w2_bf[a, b] = sb("w2_bf%d%d" % (a, b), [P, K_PASS, PACK], BF16, tag="w2_bf", bufs=2)
+            copy(
+                w2_bf[a, b][:].rearrange("p (t m) j -> p m j t", t=PACK),
+                w2_raw[a, b][:].rearrange("p j (m t) -> p m j t", t=PACK),
+            )
+
+        def quantize_w2(a, b):
+            w2_q[a, b] = quantize("w2_%d%d" % (a, b), w2_bf[a, b], K_PASS)
+
+        round_w2(0, 0, nc.scalar.copy)
+        round_w2(1, 0, nc.scalar.copy)
+
+        h_sb = {}
+        gate = {(b, half): sb("gate%d%d" % (b, half), [P, PACK, HALF], F32, tag="gate", bufs=4) for half in two for b in two}
+
+        def look(b, t, half):
+            nc.scalar.activation(
+                out=gate[b, half][:, t, :],
+                in_=h_sb[b, t][:].indirect(offs2_sb[:, 16 * half : 16 * half + 16]),
+                func=ACT.Sigmoid,
+                bias=thr_sb[:, b, t : t + 1],
+            )
+
+        y_bf = {}
+        y_q = {}
+
+        def gate_pattern(b, half):
+            y_bf[b, half] = sb("y_bf%d%d" % (b, half), [P, HALF, PACK], BF16, tag="grouped", bufs=4)
+            nc.vector.tensor_tensor(
+                y_bf[b, half][:].rearrange("p (c i) t -> p c t i", i=4),
+                gate[b, half][:].rearrange("p t (c i) -> p c t i", i=4),
+                pat_sb[b, half][:].rearrange("p t (c i) -> p c t i", i=4),
+                MULT,
+            )
+
+        def quantize_y(b, half):
+            y_q[b, half] = quantize("y_%d%d" % (b, half), y_bf[b, half], HALF)
+
+        for b in two:
+            for t in four:
+                h_sb[b, t] = sb("h_sb%d%d" % (b, t), [P, S], F32)
+                cols = slice(t * P, (t + 1) * P)
+                for s in two:
+                    acc = psum.tile([P, BANK], F32, name="acc")
+                    for a in two:
+                        nc.tensor.matmul_mx(
+                            out=acc[:],
+                            lhsT=w1_sb[b][:, a, cols].bitcast(FP4X4),
+                            lhsT_scale=w1_scale_sb[b][:, a, cols],
+                            rhs=picked[a, s][:].bitcast(FP8X4),
+                            rhs_scale=picked_planes[:, a, s * BANK : (s + 1) * BANK],
+                            start=(a == 0),
+                            stop=(a == 1),
+                        )
+                    if s == 0 or (b, t) == (0, 0):
+                        nc.vector.tensor_copy(h_sb[b, t][:, s * BANK : (s + 1) * BANK], acc[:])
+                    else:
+                        nc.scalar.copy(h_sb[b, t][:, s * BANK : (s + 1) * BANK], acc[:])
+                look(b, t, 0)
+            if b == 0:
+                quantize_w2(0, 0)
+                quantize_w2(1, 0)
+                gate_pattern(0, 0)
+                round_w2(0, 1, nc.vector.tensor_copy)
+                quantize_y(0, 0)
+        for b in two:
+            for t in four:
+                look(b, t, 1)
+        gate_pattern(1, 0)
+        quantize_w2(0, 1)
+        quantize_y(1, 0)
+        round_w2(1, 1, nc.vector.tensor_copy)
+        gate_pattern(0, 1)
+        quantize_w2(1, 1)
+        quantize_y(0, 1)
+        gate_pattern(1, 1)
+
+        w3_bf = {}
+        w3_q = {}
+
+        def round_w3(a):
+            w3_bf[a] = sb("w3_bf%d" % a, [P, N, PACK], BF16)
+            nc.vector.tensor_copy(
+                w3_bf[a][:].rearrange("p (c i) j -> p c j i", i=4),
+                w3_raw[a][:].rearrange("p j (c i) -> p c j i", i=4),
+            )
+
+        round_w3(0)
+        quantize_y(1, 1)
+        round_w3(1)
+        for a in two:
+            w3_q[a] = quantize("w3_%d" % a, w3_bf[a], N)
+
+        act = {}
+        f_bf = {}
+        f_q = {}
+
+        def hidden(b, half):
+            act[b, half] = sb("act%d%d" % (b, half), [P, PACK, HALF], F32, tag="gate", bufs=4)
+            for pair in two:
+                acc = psum.tile([P, 2, HALF], F32, name="acc")
+                for u in two:
+                    t = 2 * pair + u
+                    cols = slice(t * P, (t + 1) * P)
+                    for a in two:
+                        nc.tensor.matmul_mx(
+                            out=acc[:, u, :],
+                            lhsT=w2_q[a, b][0][:, cols].bitcast(FP8X4),
+                            lhsT_scale=w2_q[a, b][1][:, cols],
+                            rhs=y_q[a, half][0][:].bitcast(FP8X4),
+                            rhs_scale=y_q[a, half][1][:],
+                            start=(a == 0),
+                            stop=(a == 1),
+                        )
+                for u in two:
+                    t = 2 * pair + u
+                    nc.scalar.activation(
+                        out=act[b, half][:, t, :], in_=acc[:, u, :], func=ACT.Gelu_apprx_tanh, bias=b2_sb[:, b, t : t + 1]
+                    )
+
+        def apply_gain(b, half):
+            f_bf[b, half] = sb("f_bf%d%d" % (b, half), [P, HALF, PACK], BF16, tag="grouped", bufs=4)
+            nc.vector.tensor_tensor(
+                f_bf[b, half][:].rearrange("p (c i) t -> p c t i", i=4),
+                act[b, half][:].rearrange("p t (c i) -> p c t i", i=4),
+                gain_sb[:, b, :].unsqueeze(1).unsqueeze(3).to_broadcast([P, HALF // 4, PACK, 4]),
+                MULT,
+            )
+
+        def quantize_f(b, half):
+            f_q[b, half] = quantize("f_%d%d" % (b, half), f_bf[b, half], HALF)
+
+        def features(half):
+            accs = [psum.tile([P, HALF], F32, name="acc") for n in range(N_TILES)]
+            steps = [((w4_sb[:, a, :], w4_scale_sb[:, a, :]), y_q[a, half]) for a in two]
+            steps += [((w3_q[a][0][:], w3_q[a][1][:]), f_q[a, half]) for a in two]
+            for step, (weights, moving) in enumerate(steps):
+                for n in range(N_TILES):
+                    cols = slice(n * P, (n + 1) * P)
+                    nc.tensor.matmul_mx(
+                        out=accs[n][:],
+                        lhsT=weights[0][:, cols].bitcast(FP8X4),
+                        lhsT_scale=weights[1][:, cols],
+                        rhs=moving[0][:].bitcast(FP8X4),
+                        rhs_scale=moving[1][:],
+                        start=(step == 0),
+                        stop=(step == len(steps) - 1),
+                    )
+            for n in range(N_TILES):
+                result = sb("result%d%d" % (half, n), [P, HALF], F32)
+                copy = nc.vector.tensor_copy if (half, n) == (1, 1) else nc.scalar.copy
+                copy(result[:], accs[n][:])
+                nc.sync.dma_start(out[n * P : (n + 1) * P, half * HALF : (half + 1) * HALF], result[:])
+
+        for half in two:
+            for b in two:
+                hidden(b, half)
+        apply_gain(0, 0)
+        apply_gain(1, 0)
+        quantize_f(0, 0)
+        quantize_f(1, 0)
+        apply_gain(0, 1)
+        features(0)
+        apply_gain(1, 1)
+        quantize_f(0, 1)
+        quantize_f(1, 1)
+        features(1)

@@ -23,6 +23,9 @@ PASSES = 2
 BANK = 512
 HALF = PICKS // 2
 N_TILES = N // P
+W2_COLS = K_PASS // 2
+SCALAR_BANKS = range(8, 13)
+BANK_RINGS = {"short": 3, "long": 5}
 
 
 def tile_list_fence_section_gates_kernel(
@@ -34,7 +37,10 @@ def tile_list_fence_section_gates_kernel(
     with ExitStack() as ctx:
         lists = ctx.enter_context(tc.tile_pool(name="lists", bufs=1))
         keep = ctx.enter_context(tc.tile_pool(name="keep", bufs=1))
-        psum = ctx.enter_context(tc.psum_pool(name="psum", bufs=8))
+        psum = ctx.enter_context(tc.psum_pool(name="psum", bufs=1))
+
+        def bank(shape, tag):
+            return psum.tile(shape, F32, name=tag, tag=tag, bufs=BANK_RINGS[tag])
 
         def sb(name, shape, dtype, tag="", bufs=1):
             return keep.tile(shape, dtype, name=name, tag=tag or name, bufs=bufs, align_bytes=64)
@@ -58,12 +64,12 @@ def tile_list_fence_section_gates_kernel(
         tab_sb = [sb("tab_sb%d" % a, [P, T], U32) for a in two]
         w1_raw = [sb("w1_raw%d" % b, [P, PASSES, K_PASS], U16) for b in two]
 
-        def load_tab(a):
-            nc.sync.dma_start(tab_sb[a][:].bitcast(I32), tab_words[a].rearrange("p n t -> p (n t)").bitcast(I32))
-
         def load_w1(b):
             cols = w1_words[:, :, 2 * b * K_PASS : 2 * (b + 1) * K_PASS]
             nc.sync.dma_start(w1_raw[b][:].bitcast(I32), cols.rearrange("a p n -> p a n").bitcast(I32))
+
+        def load_tab(a):
+            nc.sync.dma_start(tab_sb[a][:].bitcast(I32), tab_words[a].rearrange("p n t -> p (n t)").bitcast(I32))
 
         load_tab(0)
         for q in four:
@@ -73,32 +79,37 @@ def tile_list_fence_section_gates_kernel(
             )
         load_w1(0)
         load_tab(1)
-        load_w1(1)
-        nc.sync.dma_start(offs2_sb[:], offs2)
-        thr_sb = sb("thr_sb", [P, PASSES, PACK], F32)
-        nc.sync.dma_start(thr_sb[:], thr.rearrange("(b p t) -> p b t", p=P, t=PACK))
 
+        nc.vector.tensor_copy(picked_scale[:], tab_scale_sb[:].indirect(offs_sb[:]))
+        for q in four:
+            nc.sync.dma_start(
+                picked_planes[32 * q : 32 * q + 4].bitcast(I32),
+                picked_scale[8 * q : 8 * q + 8, :].bitcast(I32),
+            )
         w2_raw = {}
         pat_sb = {}
 
-        def load_w2(a, b):
-            w2_raw[a, b] = sb("w2_raw%d%d" % (a, b), [P, PACK, K_PASS], F32)
-            rows = w2[a * K_PASS : (a + 1) * K_PASS, b * K_PASS : (b + 1) * K_PASS]
-            nc.sync.dma_start(w2_raw[a, b][:], rows.rearrange("(p j) c -> p j c", j=PACK))
+        def load_w2(a, b, u, tag=""):
+            w2_raw[a, b, u] = sb("w2_raw%d%d%d" % (a, b, u), [P, PACK, W2_COLS], F32, tag=tag)
+            first = b * K_PASS + u * W2_COLS
+            rows = w2[a * K_PASS : (a + 1) * K_PASS, first : first + W2_COLS]
+            nc.sync.dma_start(w2_raw[a, b, u][:], rows.rearrange("(p j) c -> p j c", j=PACK))
 
-        def load_pat(b, half):
-            pat_sb[b, half] = sb("pat_sb%d%d" % (b, half), [P, PACK, HALF], F32)
-            rows = pat[b * K_PASS : (b + 1) * K_PASS, half * HALF : (half + 1) * HALF]
-            nc.sync.dma_start(pat_sb[b, half][:], rows.rearrange("(p j) c -> p j c", j=PACK))
+        def load_pat(b):
+            pat_sb[b] = sb("pat_sb%d" % b, [P, PACK, PICKS], F32)
+            nc.sync.dma_start(pat_sb[b][:], pat[b * K_PASS : (b + 1) * K_PASS, :].rearrange("(p j) c -> p j c", j=PACK))
 
-        load_w2(0, 0)
-        load_w2(1, 0)
-        load_pat(0, 0)
-        load_pat(1, 0)
-        load_w2(0, 1)
-        load_w2(1, 1)
-        load_pat(0, 1)
-        load_pat(1, 1)
+        load_w1(1)
+        load_w2(0, 0, 0)
+        load_w2(0, 0, 1)
+        nc.sync.dma_start(offs2_sb[:], offs2)
+        thr_sb = sb("thr_sb", [P, PASSES, PACK], F32)
+        nc.sync.dma_start(thr_sb[:], thr.rearrange("(b p t) -> p b t", p=P, t=PACK))
+        for a, b in ((1, 0), (0, 1), (1, 1)):
+            for u in two:
+                load_w2(a, b, u)
+        load_pat(0)
+        load_pat(1)
         b2_sb = sb("b2_sb", [P, PASSES, PACK], F32)
         nc.sync.dma_start(b2_sb[:], b2.rearrange("(b p t) -> p b t", p=P, t=PACK))
         gain_sb = sb("gain_sb", [P, PASSES, PACK], F32)
@@ -114,12 +125,6 @@ def tile_list_fence_section_gates_kernel(
         w4_sb = sb("w4_sb", [P, PASSES, N], U32)
         nc.sync.dma_start(w4_sb[:].bitcast(I32), w4_words.rearrange("a p n t -> p a (n t)").bitcast(I32))
 
-        nc.vector.tensor_copy(picked_scale[:], tab_scale_sb[:].indirect(offs_sb[:]))
-        for q in four:
-            nc.scalar.dma_start(
-                picked_planes[32 * q : 32 * q + 4].bitcast(I32),
-                picked_scale[8 * q : 8 * q + 8, :].bitcast(I32),
-            )
         picked = {}
 
         def pick_words(a, s):
@@ -127,7 +132,7 @@ def tile_list_fence_section_gates_kernel(
             nc.vector.tensor_copy(picked[a, s][:], tab_sb[a][:].indirect(offs_sb[:, 32 * s : 32 * s + 32]))
 
         w1_sb = [sb("w1_sb%d" % b, [P, PASSES, K_PASS], U16) for b in two]
-        w1_scale_sb = [sb("w1_scale_sb%d" % b, [P, PASSES, K_PASS], U8) for b in two]
+        w1_scale_sb = {}
 
         def deal_w1_words(b):
             nc.scalar.copy(
@@ -135,8 +140,9 @@ def tile_list_fence_section_gates_kernel(
                 w1_raw[b][:].rearrange("p a (m t) -> p a t m", t=PACK),
             )
 
-        def deal_w1_scales(b):
-            nc.vector.tensor_copy(
+        def deal_w1_scales(b, copy, tag):
+            w1_scale_sb[b] = sb("w1_scale_sb%d" % b, [P, PASSES, K_PASS], U8, tag=tag)
+            copy(
                 w1_scale_sb[b][:].rearrange("p a (t m) -> p a t m", t=PACK),
                 w1_scale_raw[:, :, b * K_PASS : (b + 1) * K_PASS].rearrange("p a (m t) -> p a t m", t=PACK),
             )
@@ -144,11 +150,11 @@ def tile_list_fence_section_gates_kernel(
         pick_words(0, 0)
         pick_words(0, 1)
         deal_w1_words(0)
-        deal_w1_scales(0)
+        deal_w1_words(1)
+        deal_w1_scales(0, nc.gpsimd.tensor_copy, "")
         pick_words(1, 0)
         pick_words(1, 1)
-        deal_w1_words(1)
-        deal_w1_scales(1)
+        deal_w1_scales(1, nc.gpsimd.tensor_copy, "tab_sb1")
 
         def quantize(name, grouped, width):
             codes = sb(name + "_codes", [P, width], U32)
@@ -162,17 +168,18 @@ def tile_list_fence_section_gates_kernel(
         w2_q = {}
 
         def round_w2(a, b, copy):
-            w2_bf[a, b] = sb("w2_bf%d%d" % (a, b), [P, K_PASS, PACK], BF16, tag="w2_bf", bufs=2)
-            copy(
-                w2_bf[a, b][:].rearrange("p (t m) j -> p m j t", t=PACK),
-                w2_raw[a, b][:].rearrange("p j (m t) -> p m j t", t=PACK),
-            )
+            w2_bf[a, b] = sb("w2_bf%d%d" % (a, b), [P, K_PASS, PACK], BF16)
+            dealt = w2_bf[a, b][:].rearrange("p (t m) j -> p m j t", t=PACK)
+            for u in two:
+                copy(
+                    dealt[:, u * W2_COLS // PACK : (u + 1) * W2_COLS // PACK],
+                    w2_raw[a, b, u][:].rearrange("p j (m t) -> p m j t", t=PACK),
+                )
 
         def quantize_w2(a, b):
             w2_q[a, b] = quantize("w2_%d%d" % (a, b), w2_bf[a, b], K_PASS)
 
         round_w2(0, 0, nc.scalar.copy)
-        round_w2(1, 0, nc.scalar.copy)
 
         h_sb = {}
         gate = {(b, half): sb("gate%d%d" % (b, half), [P, PACK, HALF], F32, tag="gate", bufs=4) for half in two for b in two}
@@ -193,7 +200,7 @@ def tile_list_fence_section_gates_kernel(
             nc.vector.tensor_tensor(
                 y_bf[b, half][:].rearrange("p (c i) t -> p c t i", i=4),
                 gate[b, half][:].rearrange("p t (c i) -> p c t i", i=4),
-                pat_sb[b, half][:].rearrange("p t (c i) -> p c t i", i=4),
+                pat_sb[b][:, :, half * HALF : (half + 1) * HALF].rearrange("p t (c i) -> p c t i", i=4),
                 MULT,
             )
 
@@ -205,7 +212,8 @@ def tile_list_fence_section_gates_kernel(
                 h_sb[b, t] = sb("h_sb%d%d" % (b, t), [P, S], F32)
                 cols = slice(t * P, (t + 1) * P)
                 for s in two:
-                    acc = psum.tile([P, BANK], F32, name="acc")
+                    on_scalar = 2 * (PACK * b + t) + s in SCALAR_BANKS
+                    acc = bank([P, BANK], "long" if on_scalar else "short")
                     for a in two:
                         nc.tensor.matmul_mx(
                             out=acc[:],
@@ -216,28 +224,26 @@ def tile_list_fence_section_gates_kernel(
                             start=(a == 0),
                             stop=(a == 1),
                         )
-                    if s == 0 or (b, t) == (0, 0):
-                        nc.vector.tensor_copy(h_sb[b, t][:, s * BANK : (s + 1) * BANK], acc[:])
-                    else:
-                        nc.scalar.copy(h_sb[b, t][:, s * BANK : (s + 1) * BANK], acc[:])
+                    copy = nc.scalar.copy if on_scalar else nc.vector.tensor_copy
+                    copy(h_sb[b, t][:, s * BANK : (s + 1) * BANK], acc[:])
                 look(b, t, 0)
-            if b == 0:
-                quantize_w2(0, 0)
-                quantize_w2(1, 0)
-                gate_pattern(0, 0)
-                round_w2(0, 1, nc.vector.tensor_copy)
-                quantize_y(0, 0)
-        for b in two:
-            for t in four:
-                look(b, t, 1)
-        gate_pattern(1, 0)
-        quantize_w2(0, 1)
-        quantize_y(1, 0)
+                if b == 0:
+                    look(b, t, 1)
+        for t in four:
+            look(1, t, 1)
+        round_w2(1, 0, nc.vector.tensor_copy)
+        quantize_w2(0, 0)
+        round_w2(0, 1, nc.vector.tensor_copy)
+        quantize_w2(1, 0)
         round_w2(1, 1, nc.vector.tensor_copy)
-        gate_pattern(0, 1)
+        quantize_w2(0, 1)
+        gate_pattern(0, 0)
         quantize_w2(1, 1)
+        gate_pattern(0, 1)
+        quantize_y(0, 0)
+        gate_pattern(1, 0)
         quantize_y(0, 1)
-        gate_pattern(1, 1)
+        quantize_y(1, 0)
 
         w3_bf = {}
         w3_q = {}
@@ -250,8 +256,9 @@ def tile_list_fence_section_gates_kernel(
             )
 
         round_w3(0)
-        quantize_y(1, 1)
+        gate_pattern(1, 1)
         round_w3(1)
+        quantize_y(1, 1)
         for a in two:
             w3_q[a] = quantize("w3_%d" % a, w3_bf[a], N)
 
@@ -262,7 +269,7 @@ def tile_list_fence_section_gates_kernel(
         def hidden(b, half):
             act[b, half] = sb("act%d%d" % (b, half), [P, PACK, HALF], F32, tag="gate", bufs=4)
             for pair in two:
-                acc = psum.tile([P, 2, HALF], F32, name="acc")
+                acc = bank([P, 2, HALF], "long" if half == 0 or (b, pair) == (1, 1) else "short")
                 for u in two:
                     t = 2 * pair + u
                     cols = slice(t * P, (t + 1) * P)
@@ -295,7 +302,7 @@ def tile_list_fence_section_gates_kernel(
             f_q[b, half] = quantize("f_%d%d" % (b, half), f_bf[b, half], HALF)
 
         def features(half):
-            accs = [psum.tile([P, HALF], F32, name="acc") for n in range(N_TILES)]
+            accs = [bank([P, HALF], "long" if half == 0 else "short") for n in range(N_TILES)]
             steps = [((w4_sb[:, a, :], w4_scale_sb[:, a, :]), y_q[a, half]) for a in two]
             steps += [((w3_q[a][0][:], w3_q[a][1][:]), f_q[a, half]) for a in two]
             for step, (weights, moving) in enumerate(steps):

@@ -24,7 +24,8 @@ BANK = 512
 HALF = PICKS // 2
 N_TILES = N // P
 W2_COLS = K_PASS // 2
-SCALAR_BANKS = range(8, 13)
+SCALAR_BANKS = range(8, 16)
+LONG_BANKS = range(8, 13)
 BANK_RINGS = {"short": 3, "long": 5}
 
 
@@ -89,25 +90,24 @@ def tile_list_fence_section_gates_kernel(
         w2_raw = {}
         pat_sb = {}
 
-        def load_w2(a, b, u, tag=""):
-            w2_raw[a, b, u] = sb("w2_raw%d%d%d" % (a, b, u), [P, PACK, W2_COLS], F32, tag=tag)
-            first = b * K_PASS + u * W2_COLS
-            rows = w2[a * K_PASS : (a + 1) * K_PASS, first : first + W2_COLS]
-            nc.sync.dma_start(w2_raw[a, b, u][:], rows.rearrange("(p j) c -> p j c", j=PACK))
+        def load_w2(a, b, first, width):
+            raw = sb("w2_raw%d%d_%d" % (a, b, first), [P, PACK, width], F32)
+            w2_raw.setdefault((a, b), []).append((first, width, raw))
+            rows = w2[a * K_PASS : (a + 1) * K_PASS, b * K_PASS + first : b * K_PASS + first + width]
+            nc.sync.dma_start(raw[:], rows.rearrange("(p j) c -> p j c", j=PACK))
 
         def load_pat(b):
             pat_sb[b] = sb("pat_sb%d" % b, [P, PACK, PICKS], F32)
             nc.sync.dma_start(pat_sb[b][:], pat[b * K_PASS : (b + 1) * K_PASS, :].rearrange("(p j) c -> p j c", j=PACK))
 
         load_w1(1)
-        load_w2(0, 0, 0)
-        load_w2(0, 0, 1)
+        load_w2(0, 0, 0, W2_COLS)
+        load_w2(0, 0, W2_COLS, W2_COLS)
         nc.sync.dma_start(offs2_sb[:], offs2)
         thr_sb = sb("thr_sb", [P, PASSES, PACK], F32)
         nc.sync.dma_start(thr_sb[:], thr.rearrange("(b p t) -> p b t", p=P, t=PACK))
         for a, b in ((1, 0), (0, 1), (1, 1)):
-            for u in two:
-                load_w2(a, b, u)
+            load_w2(a, b, 0, K_PASS)
         load_pat(0)
         load_pat(1)
         b2_sb = sb("b2_sb", [P, PASSES, PACK], F32)
@@ -170,10 +170,10 @@ def tile_list_fence_section_gates_kernel(
         def round_w2(a, b, copy):
             w2_bf[a, b] = sb("w2_bf%d%d" % (a, b), [P, K_PASS, PACK], BF16)
             dealt = w2_bf[a, b][:].rearrange("p (t m) j -> p m j t", t=PACK)
-            for u in two:
+            for first, width, raw in w2_raw[a, b]:
                 copy(
-                    dealt[:, u * W2_COLS // PACK : (u + 1) * W2_COLS // PACK],
-                    w2_raw[a, b, u][:].rearrange("p j (m t) -> p m j t", t=PACK),
+                    dealt[:, first // PACK : (first + width) // PACK],
+                    raw[:].rearrange("p j (m t) -> p m j t", t=PACK),
                 )
 
         def quantize_w2(a, b):
@@ -182,12 +182,14 @@ def tile_list_fence_section_gates_kernel(
         round_w2(0, 0, nc.scalar.copy)
 
         h_sb = {}
-        gate = {(b, half): sb("gate%d%d" % (b, half), [P, PACK, HALF], F32, tag="gate", bufs=4) for half in two for b in two}
+        gate = {}
 
-        def look(b, t, half):
+        def look(b, t, first, width, tag=""):
+            if t == 0:
+                gate[b, first] = sb("gate%d_%d" % (b, first), [P, PACK, width], F32, tag=tag)
             nc.scalar.activation(
-                out=gate[b, half][:, t, :],
-                in_=h_sb[b, t][:].indirect(offs2_sb[:, 16 * half : 16 * half + 16]),
+                out=gate[b, first][:, t, :],
+                in_=h_sb[b, t][:].indirect(offs2_sb[:, first // 16 : (first + width) // 16]),
                 func=ACT.Sigmoid,
                 bias=thr_sb[:, b, t : t + 1],
             )
@@ -195,17 +197,17 @@ def tile_list_fence_section_gates_kernel(
         y_bf = {}
         y_q = {}
 
-        def gate_pattern(b, half):
-            y_bf[b, half] = sb("y_bf%d%d" % (b, half), [P, HALF, PACK], BF16, tag="grouped", bufs=4)
+        def gate_pattern(b, first, width, tag=""):
+            y_bf[b, first] = sb("y_bf%d_%d" % (b, first), [P, width, PACK], BF16, tag=tag)
             nc.vector.tensor_tensor(
-                y_bf[b, half][:].rearrange("p (c i) t -> p c t i", i=4),
-                gate[b, half][:].rearrange("p t (c i) -> p c t i", i=4),
-                pat_sb[b][:, :, half * HALF : (half + 1) * HALF].rearrange("p t (c i) -> p c t i", i=4),
+                y_bf[b, first][:].rearrange("p (c i) t -> p c t i", i=4),
+                gate[b, first][:].rearrange("p t (c i) -> p c t i", i=4),
+                pat_sb[b][:, :, first : first + width].rearrange("p t (c i) -> p c t i", i=4),
                 MULT,
             )
 
-        def quantize_y(b, half):
-            y_q[b, half] = quantize("y_%d%d" % (b, half), y_bf[b, half], HALF)
+        def quantize_y(b, first, width):
+            y_q[b, first] = quantize("y_%d_%d" % (b, first), y_bf[b, first], width)
 
         for b in two:
             for t in four:
@@ -213,7 +215,7 @@ def tile_list_fence_section_gates_kernel(
                 cols = slice(t * P, (t + 1) * P)
                 for s in two:
                     on_scalar = 2 * (PACK * b + t) + s in SCALAR_BANKS
-                    acc = bank([P, BANK], "long" if on_scalar else "short")
+                    acc = bank([P, BANK], "long" if 2 * (PACK * b + t) + s in LONG_BANKS else "short")
                     for a in two:
                         nc.tensor.matmul_mx(
                             out=acc[:],
@@ -226,24 +228,21 @@ def tile_list_fence_section_gates_kernel(
                         )
                     copy = nc.scalar.copy if on_scalar else nc.vector.tensor_copy
                     copy(h_sb[b, t][:, s * BANK : (s + 1) * BANK], acc[:])
-                look(b, t, 0)
-                if b == 0:
-                    look(b, t, 1)
-        for t in four:
-            look(1, t, 1)
+                look(b, t, 0, HALF)
+        for b, tag in enumerate(("w1_sb1", "picked11")):
+            for t in four:
+                look(b, t, HALF, HALF, tag=tag)
         round_w2(1, 0, nc.vector.tensor_copy)
         quantize_w2(0, 0)
         round_w2(0, 1, nc.vector.tensor_copy)
         quantize_w2(1, 0)
         round_w2(1, 1, nc.vector.tensor_copy)
         quantize_w2(0, 1)
-        gate_pattern(0, 0)
+        gate_pattern(0, 0, HALF)
         quantize_w2(1, 1)
-        gate_pattern(0, 1)
-        quantize_y(0, 0)
-        gate_pattern(1, 0)
-        quantize_y(0, 1)
-        quantize_y(1, 0)
+        gate_pattern(1, 0, HALF)
+        quantize_y(0, 0, HALF)
+        quantize_y(1, 0, HALF)
 
         w3_bf = {}
         w3_q = {}
@@ -256,83 +255,95 @@ def tile_list_fence_section_gates_kernel(
             )
 
         round_w3(0)
-        gate_pattern(1, 1)
         round_w3(1)
-        quantize_y(1, 1)
         for a in two:
             w3_q[a] = quantize("w3_%d" % a, w3_bf[a], N)
+        gate_pattern(0, HALF, HALF, tag="w3_raw1")
+        quantize_y(0, HALF, HALF)
+        gate_pattern(1, HALF, HALF, tag="w1_sb1")
+        quantize_y(1, HALF, HALF)
 
         act = {}
         f_bf = {}
         f_q = {}
 
-        def hidden(b, half):
-            act[b, half] = sb("act%d%d" % (b, half), [P, PACK, HALF], F32, tag="gate", bufs=4)
-            for pair in two:
-                acc = bank([P, 2, HALF], "long" if half == 0 or (b, pair) == (1, 1) else "short")
-                for u in two:
-                    t = 2 * pair + u
-                    cols = slice(t * P, (t + 1) * P)
+        def columns(pieces, b, first, width):
+            start = max(key[1] for key in pieces if key[0] == b and key[1] <= first)
+            cols = slice(first - start, first - start + width)
+            return pieces[b, start][0][:, cols].bitcast(FP8X4), pieces[b, start][1][:, cols]
+
+        def hidden(b, first, width):
+            act[b, first] = sb("act%d_%d" % (b, first), [P, PACK, width], F32, tag="h_sb%d%d" % (b, first // P))
+            per_bank = BANK // width
+            for t0 in range(0, PACK, per_bank):
+                acc = bank([P, per_bank, width], "short")
+                for u in range(per_bank):
+                    cols = slice((t0 + u) * P, (t0 + u + 1) * P)
                     for a in two:
+                        codes, scales = columns(y_q, a, first, width)
                         nc.tensor.matmul_mx(
                             out=acc[:, u, :],
                             lhsT=w2_q[a, b][0][:, cols].bitcast(FP8X4),
                             lhsT_scale=w2_q[a, b][1][:, cols],
-                            rhs=y_q[a, half][0][:].bitcast(FP8X4),
-                            rhs_scale=y_q[a, half][1][:],
+                            rhs=codes,
+                            rhs_scale=scales,
                             start=(a == 0),
                             stop=(a == 1),
                         )
-                for u in two:
-                    t = 2 * pair + u
+                for u in range(per_bank):
+                    t = t0 + u
                     nc.scalar.activation(
-                        out=act[b, half][:, t, :], in_=acc[:, u, :], func=ACT.Gelu_apprx_tanh, bias=b2_sb[:, b, t : t + 1]
+                        out=act[b, first][:, t, :], in_=acc[:, u, :], func=ACT.Gelu_apprx_tanh, bias=b2_sb[:, b, t : t + 1]
                     )
 
-        def apply_gain(b, half):
-            f_bf[b, half] = sb("f_bf%d%d" % (b, half), [P, HALF, PACK], BF16, tag="grouped", bufs=4)
+        def apply_gain(b, first, width, tag=""):
+            f_bf[b, first] = sb("f_bf%d_%d" % (b, first), [P, width, PACK], BF16, tag=tag)
             nc.vector.tensor_tensor(
-                f_bf[b, half][:].rearrange("p (c i) t -> p c t i", i=4),
-                act[b, half][:].rearrange("p t (c i) -> p c t i", i=4),
-                gain_sb[:, b, :].unsqueeze(1).unsqueeze(3).to_broadcast([P, HALF // 4, PACK, 4]),
+                f_bf[b, first][:].rearrange("p (c i) t -> p c t i", i=4),
+                act[b, first][:].rearrange("p t (c i) -> p c t i", i=4),
+                gain_sb[:, b, :].unsqueeze(1).unsqueeze(3).to_broadcast([P, width // 4, PACK, 4]),
                 MULT,
             )
 
-        def quantize_f(b, half):
-            f_q[b, half] = quantize("f_%d%d" % (b, half), f_bf[b, half], HALF)
+        def quantize_f(b, first, width):
+            f_q[b, first] = quantize("f_%d_%d" % (b, first), f_bf[b, first], width)
 
-        def features(half):
-            accs = [bank([P, HALF], "long" if half == 0 else "short") for n in range(N_TILES)]
-            steps = [((w4_sb[:, a, :], w4_scale_sb[:, a, :]), y_q[a, half]) for a in two]
-            steps += [((w3_q[a][0][:], w3_q[a][1][:]), f_q[a, half]) for a in two]
-            for step, (weights, moving) in enumerate(steps):
-                for n in range(N_TILES):
+        def features(first, width, n0, n1, tag=""):
+            acc = bank([P, n1 - n0, width], "long")
+            steps = [(w4_sb[:, a, :], w4_scale_sb[:, a, :], y_q, a) for a in two]
+            steps += [(w3_q[a][0][:], w3_q[a][1][:], f_q, a) for a in two]
+            for step, (words, planes, pieces, a) in enumerate(steps):
+                codes, scales = columns(pieces, a, first, width)
+                for n in range(n0, n1):
                     cols = slice(n * P, (n + 1) * P)
                     nc.tensor.matmul_mx(
-                        out=accs[n][:],
-                        lhsT=weights[0][:, cols].bitcast(FP8X4),
-                        lhsT_scale=weights[1][:, cols],
-                        rhs=moving[0][:].bitcast(FP8X4),
-                        rhs_scale=moving[1][:],
-                        start=(step == 0),
-                        stop=(step == len(steps) - 1),
+                        out=acc[:, n - n0, :],
+                        lhsT=words[:, cols].bitcast(FP8X4),
+                        lhsT_scale=planes[:, cols],
+                        rhs=codes,
+                        rhs_scale=scales,
+                        start=(step == 0 and n == n0),
+                        stop=(step == len(steps) - 1 and n == n1 - 1),
                     )
-            for n in range(N_TILES):
-                result = sb("result%d%d" % (half, n), [P, HALF], F32)
-                copy = nc.vector.tensor_copy if (half, n) == (1, 1) else nc.scalar.copy
-                copy(result[:], accs[n][:])
-                nc.sync.dma_start(out[n * P : (n + 1) * P, half * HALF : (half + 1) * HALF], result[:])
+            result = sb("result%d_%d" % (first, n0), [P, n1 - n0, width], F32, tag=tag)
+            nc.scalar.copy(result[:], acc[:])
+            rows = out[n0 * P : n1 * P, first : first + width]
+            nc.sync.dma_start(rows.rearrange("(n p) m -> p n m", p=P), result[:])
 
-        for half in two:
-            for b in two:
-                hidden(b, half)
-        apply_gain(0, 0)
-        apply_gain(1, 0)
-        quantize_f(0, 0)
-        quantize_f(1, 0)
-        apply_gain(0, 1)
-        features(0)
-        apply_gain(1, 1)
-        quantize_f(0, 1)
-        quantize_f(1, 1)
-        features(1)
+        pieces = [(0, 0, HALF), (1, 0, HALF), (0, HALF, HALF), (1, HALF, P), (1, HALF + P, P)]
+        for piece in pieces:
+            hidden(*piece)
+        apply_gain(*pieces[0], tag="picked11")
+        apply_gain(*pieces[1], tag="pat_sb1")
+        quantize_f(*pieces[0])
+        quantize_f(*pieces[1])
+        apply_gain(*pieces[2])
+        features(0, HALF, 0, 2, tag="b2_sb")
+        apply_gain(*pieces[3])
+        features(0, HALF, 2, 3, tag="h_sb12")
+        quantize_f(*pieces[2])
+        apply_gain(*pieces[4])
+        quantize_f(*pieces[3])
+        features(HALF, P, 0, 3)
+        quantize_f(*pieces[4])
+        features(HALF + P, P, 0, 3)

@@ -15,6 +15,7 @@ FP8X4 = mybir.dt.float8_e4m3fn_x4
 FP4X4 = mybir.dt.float4_e2m1fn_x4
 ACT = mybir.ActivationFunctionType
 MULT = mybir.AluOpType.mult
+ADD = mybir.AluOpType.add
 
 P = 128
 PACK = 4
@@ -24,8 +25,8 @@ BANK = 512
 HALF = PICKS // 2
 N_TILES = N // P
 W2_COLS = K_PASS // 2
-SCALAR_BANKS = range(8, 16)
-LONG_BANKS = range(8, 13)
+SCALAR_BANKS = range(10, 16)
+LONG_BANKS = range(10, 16)
 BANK_RINGS = {"short": 3, "long": 5}
 
 
@@ -106,17 +107,18 @@ def tile_list_fence_section_gates_kernel(
         nc.sync.dma_start(offs2_sb[:], offs2)
         thr_sb = sb("thr_sb", [P, PASSES, PACK], F32)
         nc.sync.dma_start(thr_sb[:], thr.rearrange("(b p t) -> p b t", p=P, t=PACK))
-        for a, b in ((1, 0), (0, 1), (1, 1)):
-            load_w2(a, b, 0, K_PASS)
+        w3_raw = [sb("w3_raw%d" % a, [P, PACK, N], F32) for a in two]
+        for a in two:
+            nc.sync.dma_start(w3_raw[a][:], w3[a * K_PASS : (a + 1) * K_PASS, :].rearrange("(p j) c -> p j c", j=PACK))
+        load_w2(1, 0, 0, K_PASS)
+        load_w2(0, 1, 0, K_PASS)
         load_pat(0)
+        load_w2(1, 1, 0, K_PASS)
         load_pat(1)
         b2_sb = sb("b2_sb", [P, PASSES, PACK], F32)
         nc.sync.dma_start(b2_sb[:], b2.rearrange("(b p t) -> p b t", p=P, t=PACK))
         gain_sb = sb("gain_sb", [P, PASSES, PACK], F32)
         nc.sync.dma_start(gain_sb[:], gain.rearrange("(b p t) -> p b t", p=P, t=PACK))
-        w3_raw = [sb("w3_raw%d" % a, [P, PACK, N], F32) for a in two]
-        for a in two:
-            nc.sync.dma_start(w3_raw[a][:], w3[a * K_PASS : (a + 1) * K_PASS, :].rearrange("(p j) c -> p j c", j=PACK))
         for q in four:
             nc.sync.dma_start(
                 w4_scale_sb[32 * q : 32 * q + 4].bitcast(I32),
@@ -156,8 +158,8 @@ def tile_list_fence_section_gates_kernel(
         pick_words(1, 1)
         deal_w1_scales(1, nc.gpsimd.tensor_copy, "tab_sb1")
 
-        def quantize(name, grouped, width):
-            codes = sb(name + "_codes", [P, width], U32)
+        def quantize(name, grouped, width, tag=""):
+            codes = sb(name + "_codes", [P, width], U32, tag=tag)
             scales = sb(name + "_scales", [P, width], U8)
             nc.vector.quantize_mx(
                 out=codes[:].bitcast(FP8X4), scales=scales[:], in_=grouped[:].rearrange("p c j -> p (c j)")
@@ -167,8 +169,8 @@ def tile_list_fence_section_gates_kernel(
         w2_bf = {}
         w2_q = {}
 
-        def round_w2(a, b, copy):
-            w2_bf[a, b] = sb("w2_bf%d%d" % (a, b), [P, K_PASS, PACK], BF16)
+        def round_w2(a, b, copy, tag=""):
+            w2_bf[a, b] = sb("w2_bf%d%d" % (a, b), [P, K_PASS, PACK], BF16, tag=tag)
             dealt = w2_bf[a, b][:].rearrange("p (t m) j -> p m j t", t=PACK)
             for first, width, raw in w2_raw[a, b]:
                 copy(
@@ -176,10 +178,14 @@ def tile_list_fence_section_gates_kernel(
                     raw[:].rearrange("p j (m t) -> p m j t", t=PACK),
                 )
 
-        def quantize_w2(a, b):
-            w2_q[a, b] = quantize("w2_%d%d" % (a, b), w2_bf[a, b], K_PASS)
+        def quantize_w2(a, b, tag=""):
+            w2_q[a, b] = quantize("w2_%d%d" % (a, b), w2_bf[a, b], K_PASS, tag=tag)
 
         round_w2(0, 0, nc.scalar.copy)
+
+        w3_bf = [sb("w3_bf%d" % a, [P, N, PACK], BF16) for a in two]
+        for a in two:
+            nc.gpsimd.tensor_scalar(w3_bf[a][:], w3_raw[a][:].rearrange("p j c -> p c j"), 1.0, 0.0, MULT, ADD)
 
         h_sb = {}
         gate = {}
@@ -199,9 +205,10 @@ def tile_list_fence_section_gates_kernel(
 
         def gate_pattern(b, first, width, tag=""):
             y_bf[b, first] = sb("y_bf%d_%d" % (b, first), [P, width, PACK], BF16, tag=tag)
+            opened = gate[0, 0][:, :, first : first + width] if b == 0 else gate[b, first][:]
             nc.vector.tensor_tensor(
                 y_bf[b, first][:].rearrange("p (c i) t -> p c t i", i=4),
-                gate[b, first][:].rearrange("p t (c i) -> p c t i", i=4),
+                opened.rearrange("p t (c i) -> p c t i", i=4),
                 pat_sb[b][:, :, first : first + width].rearrange("p t (c i) -> p c t i", i=4),
                 MULT,
             )
@@ -228,39 +235,25 @@ def tile_list_fence_section_gates_kernel(
                         )
                     copy = nc.scalar.copy if on_scalar else nc.vector.tensor_copy
                     copy(h_sb[b, t][:, s * BANK : (s + 1) * BANK], acc[:])
-                look(b, t, 0, HALF)
-        for b, tag in enumerate(("w1_sb1", "picked11")):
-            for t in four:
-                look(b, t, HALF, HALF, tag=tag)
-        round_w2(1, 0, nc.vector.tensor_copy)
-        quantize_w2(0, 0)
-        round_w2(0, 1, nc.vector.tensor_copy)
+                look(b, t, 0, PICKS if b == 0 else HALF)
+        for t in four:
+            look(1, t, HALF, HALF, tag="picked11")
+        round_w2(1, 0, nc.vector.tensor_copy, tag="w1_sb0")
+        w3_q = [quantize("w3_0", w3_bf[0], N, tag="w1_scale_sb0")]
+        quantize_w2(0, 0, tag="w3_bf0")
+        w3_q.append(quantize("w3_1", w3_bf[1], N, tag="w2_bf00"))
         quantize_w2(1, 0)
-        round_w2(1, 1, nc.vector.tensor_copy)
-        quantize_w2(0, 1)
+        round_w2(0, 1, nc.vector.tensor_copy)
         gate_pattern(0, 0, HALF)
-        quantize_w2(1, 1)
-        gate_pattern(1, 0, HALF)
+        quantize_w2(0, 1)
+        round_w2(1, 1, nc.vector.tensor_copy)
         quantize_y(0, 0, HALF)
+        gate_pattern(1, 0, HALF)
+        quantize_w2(1, 1)
         quantize_y(1, 0, HALF)
-
-        w3_bf = {}
-        w3_q = {}
-
-        def round_w3(a):
-            w3_bf[a] = sb("w3_bf%d" % a, [P, N, PACK], BF16)
-            nc.vector.tensor_copy(
-                w3_bf[a][:].rearrange("p (c i) j -> p c j i", i=4),
-                w3_raw[a][:].rearrange("p j (c i) -> p c j i", i=4),
-            )
-
-        round_w3(0)
-        round_w3(1)
-        for a in two:
-            w3_q[a] = quantize("w3_%d" % a, w3_bf[a], N)
-        gate_pattern(0, HALF, HALF, tag="w3_raw1")
+        gate_pattern(0, HALF, HALF, tag="gate1_0")
+        gate_pattern(1, HALF, HALF, tag="gate0_0")
         quantize_y(0, HALF, HALF)
-        gate_pattern(1, HALF, HALF, tag="w1_sb1")
         quantize_y(1, HALF, HALF)
 
         act = {}
@@ -276,7 +269,7 @@ def tile_list_fence_section_gates_kernel(
             act[b, first] = sb("act%d_%d" % (b, first), [P, PACK, width], F32, tag="h_sb%d%d" % (b, first // P))
             per_bank = BANK // width
             for t0 in range(0, PACK, per_bank):
-                acc = bank([P, per_bank, width], "short")
+                acc = bank([P, per_bank, width], "short" if HALF <= first < PICKS - P else "long")
                 for u in range(per_bank):
                     cols = slice((t0 + u) * P, (t0 + u + 1) * P)
                     for a in two:
@@ -308,7 +301,7 @@ def tile_list_fence_section_gates_kernel(
         def quantize_f(b, first, width):
             f_q[b, first] = quantize("f_%d_%d" % (b, first), f_bf[b, first], width)
 
-        def features(first, width, n0, n1, tag=""):
+        def features(first, width, n0, n1, copy=nc.scalar.copy):
             acc = bank([P, n1 - n0, width], "long")
             steps = [(w4_sb[:, a, :], w4_scale_sb[:, a, :], y_q, a) for a in two]
             steps += [(w3_q[a][0][:], w3_q[a][1][:], f_q, a) for a in two]
@@ -325,8 +318,8 @@ def tile_list_fence_section_gates_kernel(
                         start=(step == 0 and n == n0),
                         stop=(step == len(steps) - 1 and n == n1 - 1),
                     )
-            result = sb("result%d_%d" % (first, n0), [P, n1 - n0, width], F32, tag=tag)
-            nc.scalar.copy(result[:], acc[:])
+            result = sb("result%d_%d" % (first, n0), [P, n1 - n0, width], F32)
+            copy(result[:], acc[:])
             rows = out[n0 * P : n1 * P, first : first + width]
             nc.sync.dma_start(rows.rearrange("(n p) m -> p n m", p=P), result[:])
 
@@ -338,12 +331,12 @@ def tile_list_fence_section_gates_kernel(
         quantize_f(*pieces[0])
         quantize_f(*pieces[1])
         apply_gain(*pieces[2])
-        features(0, HALF, 0, 2, tag="b2_sb")
+        features(0, HALF, 0, 2)
+        features(0, HALF, 2, 3)
         apply_gain(*pieces[3])
-        features(0, HALF, 2, 3, tag="h_sb12")
         quantize_f(*pieces[2])
         apply_gain(*pieces[4])
         quantize_f(*pieces[3])
         features(HALF, P, 0, 3)
         quantize_f(*pieces[4])
-        features(HALF + P, P, 0, 3)
+        features(HALF + P, P, 0, 3, copy=nc.vector.tensor_copy)

@@ -113,8 +113,8 @@ def tile_list_fence_section_gates_kernel(
         load_w2(1, 0, 0, K_PASS)
         load_w2(0, 1, 0, K_PASS)
         load_pat(0)
-        load_w2(1, 1, 0, K_PASS)
         load_pat(1)
+        load_w2(1, 1, 0, K_PASS)
         b2_sb = sb("b2_sb", [P, PASSES, PACK], F32)
         nc.sync.dma_start(b2_sb[:], b2.rearrange("(b p t) -> p b t", p=P, t=PACK))
         gain_sb = sb("gain_sb", [P, PASSES, PACK], F32)
@@ -142,21 +142,22 @@ def tile_list_fence_section_gates_kernel(
                 w1_raw[b][:].rearrange("p a (m t) -> p a t m", t=PACK),
             )
 
-        def deal_w1_scales(b, copy, tag):
-            w1_scale_sb[b] = sb("w1_scale_sb%d" % b, [P, PASSES, K_PASS], U8, tag=tag)
-            copy(
-                w1_scale_sb[b][:].rearrange("p a (t m) -> p a t m", t=PACK),
-                w1_scale_raw[:, :, b * K_PASS : (b + 1) * K_PASS].rearrange("p a (m t) -> p a t m", t=PACK),
-            )
+        def deal_w1_scales(name, b, t0, t1, copy, tag=""):
+            dealt = sb(name, [P, PASSES, t1 - t0, P], U8, tag=tag)
+            cols = w1_scale_raw[:, :, b * K_PASS : (b + 1) * K_PASS].rearrange("p a (m t) -> p a t m", t=PACK)
+            copy(dealt[:], cols[:, :, t0:t1, :])
+            for t in range(t0, t1):
+                w1_scale_sb[b, t] = dealt[:, :, t - t0, :]
 
         pick_words(0, 0)
         pick_words(0, 1)
         deal_w1_words(0)
         deal_w1_words(1)
-        deal_w1_scales(0, nc.gpsimd.tensor_copy, "")
+        deal_w1_scales("w1_scale_first", 0, 0, 1, nc.vector.tensor_copy)
+        deal_w1_scales("w1_scale_sb0", 0, 1, PACK, nc.gpsimd.tensor_copy)
         pick_words(1, 0)
         pick_words(1, 1)
-        deal_w1_scales(1, nc.gpsimd.tensor_copy, "tab_sb1")
+        deal_w1_scales("w1_scale_sb1", 1, 0, PACK, nc.gpsimd.tensor_copy, tag="tab_sb1")
 
         def quantize(name, grouped, width, tag=""):
             codes = sb(name + "_codes", [P, width], U32, tag=tag)
@@ -227,7 +228,7 @@ def tile_list_fence_section_gates_kernel(
                         nc.tensor.matmul_mx(
                             out=acc[:],
                             lhsT=w1_sb[b][:, a, cols].bitcast(FP4X4),
-                            lhsT_scale=w1_scale_sb[b][:, a, cols],
+                            lhsT_scale=w1_scale_sb[b, t][:, a, :],
                             rhs=picked[a, s][:].bitcast(FP8X4),
                             rhs_scale=picked_planes[:, a, s * BANK : (s + 1) * BANK],
                             start=(a == 0),
@@ -246,14 +247,14 @@ def tile_list_fence_section_gates_kernel(
         round_w2(0, 1, nc.vector.tensor_copy)
         gate_pattern(0, 0, HALF)
         quantize_w2(0, 1)
-        round_w2(1, 1, nc.vector.tensor_copy)
+        gate_pattern(0, HALF, HALF)
         quantize_y(0, 0, HALF)
-        gate_pattern(1, 0, HALF)
-        quantize_w2(1, 1)
-        quantize_y(1, 0, HALF)
-        gate_pattern(0, HALF, HALF, tag="gate1_0")
-        gate_pattern(1, HALF, HALF, tag="gate0_0")
         quantize_y(0, HALF, HALF)
+        gate_pattern(1, 0, HALF)
+        round_w2(1, 1, nc.vector.tensor_copy, tag="gate1_0")
+        quantize_y(1, 0, HALF)
+        quantize_w2(1, 1)
+        gate_pattern(1, HALF, HALF, tag="w2_raw11_0")
         quantize_y(1, HALF, HALF)
 
         act = {}

from contextlib import ExitStack

import concourse.mybir as mybir

K, T, S, H, PICKS, M, N = 1024, 2048, 1024, 1024, 512, 1024, 384
FLOPS = 2 * (K * H * S + H * M * PICKS + M * N * PICKS + H * N * PICKS)

F32 = mybir.dt.float32
BF16 = mybir.dt.bfloat16
I32 = mybir.dt.int32
U32 = mybir.dt.uint32
U16 = mybir.dt.uint16
U8 = mybir.dt.uint8
FP8X4 = mybir.dt.float8_e4m3fn_x4
FP4X4 = mybir.dt.float4_e2m1fn_x4
ACT = mybir.ActivationFunctionType
MULT = mybir.AluOpType.mult
ADD = mybir.AluOpType.add

P = 128
PACK = 4
K_PASS = P * PACK
PASSES = 2
BANK = 512
HALF = PICKS // 2
N_TILES = N // P
W2_COLS = K_PASS // 2
SCALAR_BANKS = range(10, 16)
LONG_BANKS = range(10, 16)
BANK_RINGS = {"short": 3, "long": 5}


def tile_list_fence_section_gates_kernel(
    tc, tab_words, tab_scales, offs, w1_words, w1_scales, offs2, thr, pat, w2, b2, gain, w3, w4_words, w4_scales, out
):
    nc = tc.nc
    two = range(2)
    four = range(PACK)
    with ExitStack() as ctx:
        lists = ctx.enter_context(tc.tile_pool(name="lists", bufs=1))
        keep = ctx.enter_context(tc.tile_pool(name="keep", bufs=1))
        psum = ctx.enter_context(tc.psum_pool(name="psum", bufs=1))

        def bank(shape, tag):
            return psum.tile(shape, F32, name=tag, tag=tag, bufs=BANK_RINGS[tag])

        def sb(name, shape, dtype, tag="", bufs=1):
            return keep.tile(shape, dtype, name=name, tag=tag or name, bufs=bufs, align_bytes=64)

        offs_sb = lists.tile([P, S // 16], U16, name="offs_sb")
        offs2_sb = lists.tile([P, PICKS // 16], U16, name="offs2_sb")

        tab_scale_sb = sb("tab_scale_sb", [P, T], U8)
        w1_scale_raw = sb("w1_scale_raw", [P, PASSES, H], U8)
        picked_scale = sb("picked_scale", [P, S], U8)
        picked_planes = sb("picked_planes", [P, PASSES, S], U8)
        w4_scale_sb = sb("w4_scale_sb", [P, PASSES, N], U8)
        nc.vector.memset(tab_scale_sb[32:64, :].bitcast(I32), 0)
        nc.vector.memset(tab_scale_sb[64:128, :].bitcast(I32), 0)
        nc.gpsimd.memset(w1_scale_raw[:].bitcast(I32), 0)
        nc.gpsimd.memset(picked_planes[:].bitcast(I32), 0)
        nc.gpsimd.memset(w4_scale_sb[:].bitcast(I32), 0)

        nc.sync.dma_start(offs_sb[:], offs)
        nc.sync.dma_start(tab_scale_sb[0:32, :].bitcast(I32), tab_scales.rearrange("a r n -> r a n").bitcast(I32))
        tab_sb = [sb("tab_sb%d" % a, [P, T], U32) for a in two]
        w1_raw = [sb("w1_raw%d" % b, [P, PASSES, K_PASS], U16) for b in two]

        def load_w1(b):
            cols = w1_words[:, :, 2 * b * K_PASS : 2 * (b + 1) * K_PASS]
            nc.sync.dma_start(w1_raw[b][:].bitcast(I32), cols.rearrange("a p n -> p a n").bitcast(I32))

        def load_tab(a):
            nc.sync.dma_start(tab_sb[a][:].bitcast(I32), tab_words[a].rearrange("p n t -> p (n t)").bitcast(I32))

        load_tab(0)
        for q in four:
            nc.sync.dma_start(
                w1_scale_raw[32 * q : 32 * q + 4].bitcast(I32),
                w1_scales[:, 4 * q : 4 * q + 4, :].rearrange("a r n -> r a n").bitcast(I32),
            )
        load_w1(0)
        load_tab(1)

        nc.vector.tensor_copy(picked_scale[:], tab_scale_sb[:].indirect(offs_sb[:]))
        for q in four:
            nc.sync.dma_start(
                picked_planes[32 * q : 32 * q + 4].bitcast(I32),
                picked_scale[8 * q : 8 * q + 8, :].bitcast(I32),
            )
        w2_raw = {}
        pat_sb = {}

        def load_w2(a, b, first, width):
            raw = sb("w2_raw%d%d_%d" % (a, b, first), [P, PACK, width], F32)
            w2_raw.setdefault((a, b), []).append((first, width, raw))
            rows = w2[a * K_PASS : (a + 1) * K_PASS, b * K_PASS + first : b * K_PASS + first + width]
            nc.sync.dma_start(raw[:], rows.rearrange("(p j) c -> p j c", j=PACK))

        def load_pat(b):
            pat_sb[b] = sb("pat_sb%d" % b, [P, PACK, PICKS], F32)
            nc.sync.dma_start(pat_sb[b][:], pat[b * K_PASS : (b + 1) * K_PASS, :].rearrange("(p j) c -> p j c", j=PACK))

        load_w1(1)
        load_w2(0, 0, 0, W2_COLS)
        load_w2(0, 0, W2_COLS, W2_COLS)
        nc.sync.dma_start(offs2_sb[:], offs2)
        thr_sb = sb("thr_sb", [P, PASSES, PACK], F32)
        nc.sync.dma_start(thr_sb[:], thr.rearrange("(b p t) -> p b t", p=P, t=PACK))
        w3_raw = [sb("w3_raw%d" % a, [P, PACK, N], F32) for a in two]
        for a in two:
            nc.sync.dma_start(w3_raw[a][:], w3[a * K_PASS : (a + 1) * K_PASS, :].rearrange("(p j) c -> p j c", j=PACK))
        load_w2(1, 0, 0, K_PASS)
        load_w2(0, 1, 0, K_PASS)
        load_pat(0)
        load_pat(1)
        load_w2(1, 1, 0, K_PASS)
        b2_sb = sb("b2_sb", [P, PASSES, PACK], F32)
        nc.sync.dma_start(b2_sb[:], b2.rearrange("(b p t) -> p b t", p=P, t=PACK))
        gain_sb = sb("gain_sb", [P, PASSES, PACK], F32)
        nc.sync.dma_start(gain_sb[:], gain.rearrange("(b p t) -> p b t", p=P, t=PACK))
        for q in four:
            nc.sync.dma_start(
                w4_scale_sb[32 * q : 32 * q + 4].bitcast(I32),
                w4_scales[:, 4 * q : 4 * q + 4, :].rearrange("a r n -> r a n").bitcast(I32),
            )
        w4_sb = sb("w4_sb", [P, PASSES, N], U32)
        nc.sync.dma_start(w4_sb[:].bitcast(I32), w4_words.rearrange("a p n t -> p a (n t)").bitcast(I32))

        picked = {}

        def pick_words(a, s):
            picked[a, s] = sb("picked%d%d" % (a, s), [P, BANK], U32)
            nc.vector.tensor_copy(picked[a, s][:], tab_sb[a][:].indirect(offs_sb[:, 32 * s : 32 * s + 32]))

        w1_sb = [sb("w1_sb%d" % b, [P, PASSES, K_PASS], U16) for b in two]
        w1_scale_sb = {}

        def deal_w1_words(b):
            nc.scalar.copy(
                w1_sb[b][:].rearrange("p a (t m) -> p a t m", t=PACK),
                w1_raw[b][:].rearrange("p a (m t) -> p a t m", t=PACK),
            )

        def deal_w1_scales(name, b, t0, t1, copy, tag=""):
            dealt = sb(name, [P, PASSES, t1 - t0, P], U8, tag=tag)
            cols = w1_scale_raw[:, :, b * K_PASS : (b + 1) * K_PASS].rearrange("p a (m t) -> p a t m", t=PACK)
            copy(dealt[:], cols[:, :, t0:t1, :])
            for t in range(t0, t1):
                w1_scale_sb[b, t] = dealt[:, :, t - t0, :]

        pick_words(0, 0)
        pick_words(0, 1)
        deal_w1_words(0)
        deal_w1_words(1)
        deal_w1_scales("w1_scale_first", 0, 0, 1, nc.vector.tensor_copy)
        deal_w1_scales("w1_scale_sb0", 0, 1, PACK, nc.gpsimd.tensor_copy)
        pick_words(1, 0)
        pick_words(1, 1)
        deal_w1_scales("w1_scale_sb1", 1, 0, PACK, nc.gpsimd.tensor_copy, tag="tab_sb1")

        def quantize(name, grouped, width, tag=""):
            codes = sb(name + "_codes", [P, width], U32, tag=tag)
            scales = sb(name + "_scales", [P, width], U8)
            nc.vector.quantize_mx(
                out=codes[:].bitcast(FP8X4), scales=scales[:], in_=grouped[:].rearrange("p c j -> p (c j)")
            )
            return codes, scales

        w2_bf = {}
        w2_q = {}

        def round_w2(a, b, copy, tag=""):
            w2_bf[a, b] = sb("w2_bf%d%d" % (a, b), [P, K_PASS, PACK], BF16, tag=tag)
            dealt = w2_bf[a, b][:].rearrange("p (t m) j -> p m j t", t=PACK)
            for first, width, raw in w2_raw[a, b]:
                copy(
                    dealt[:, first // PACK : (first + width) // PACK],
                    raw[:].rearrange("p j (m t) -> p m j t", t=PACK),
                )

        def quantize_w2(a, b, tag=""):
            w2_q[a, b] = quantize("w2_%d%d" % (a, b), w2_bf[a, b], K_PASS, tag=tag)

        round_w2(0, 0, nc.scalar.copy)

        w3_bf = [sb("w3_bf%d" % a, [P, N, PACK], BF16) for a in two]
        for a in two:
            nc.gpsimd.tensor_scalar(w3_bf[a][:], w3_raw[a][:].rearrange("p j c -> p c j"), 1.0, 0.0, MULT, ADD)

        h_sb = {}
        gate = {}

        def look(b, t, first, width, tag=""):
            if t == 0:
                gate[b, first] = sb("gate%d_%d" % (b, first), [P, PACK, width], F32, tag=tag)
            nc.scalar.activation(
                out=gate[b, first][:, t, :],
                in_=h_sb[b, t][:].indirect(offs2_sb[:, first // 16 : (first + width) // 16]),
                func=ACT.Sigmoid,
                bias=thr_sb[:, b, t : t + 1],
            )

        y_bf = {}
        y_q = {}

        def gate_pattern(b, first, width, tag=""):
            y_bf[b, first] = sb("y_bf%d_%d" % (b, first), [P, width, PACK], BF16, tag=tag)
            opened = gate[0, 0][:, :, first : first + width] if b == 0 else gate[b, first][:]
            nc.vector.tensor_tensor(
                y_bf[b, first][:].rearrange("p (c i) t -> p c t i", i=4),
                opened.rearrange("p t (c i) -> p c t i", i=4),
                pat_sb[b][:, :, first : first + width].rearrange("p t (c i) -> p c t i", i=4),
                MULT,
            )

        def quantize_y(b, first, width):
            y_q[b, first] = quantize("y_%d_%d" % (b, first), y_bf[b, first], width)

        for b in two:
            for t in four:
                h_sb[b, t] = sb("h_sb%d%d" % (b, t), [P, S], F32)
                cols = slice(t * P, (t + 1) * P)
                for s in two:
                    on_scalar = 2 * (PACK * b + t) + s in SCALAR_BANKS
                    acc = bank([P, BANK], "long" if 2 * (PACK * b + t) + s in LONG_BANKS else "short")
                    for a in two:
                        nc.tensor.matmul_mx(
                            out=acc[:],
                            lhsT=w1_sb[b][:, a, cols].bitcast(FP4X4),
                            lhsT_scale=w1_scale_sb[b, t][:, a, :],
                            rhs=picked[a, s][:].bitcast(FP8X4),
                            rhs_scale=picked_planes[:, a, s * BANK : (s + 1) * BANK],
                            start=(a == 0),
                            stop=(a == 1),
                        )
                    copy = nc.scalar.copy if on_scalar else nc.vector.tensor_copy
                    copy(h_sb[b, t][:, s * BANK : (s + 1) * BANK], acc[:])
                look(b, t, 0, PICKS if b == 0 else HALF)
        for t in four:
            look(1, t, HALF, HALF, tag="picked11")
        round_w2(1, 0, nc.vector.tensor_copy, tag="w1_sb0")
        w3_q = [quantize("w3_0", w3_bf[0], N, tag="w1_scale_sb0")]
        quantize_w2(0, 0, tag="w3_bf0")
        w3_q.append(quantize("w3_1", w3_bf[1], N, tag="w2_bf00"))
        quantize_w2(1, 0)
        round_w2(0, 1, nc.vector.tensor_copy)
        gate_pattern(0, 0, HALF)
        quantize_w2(0, 1)
        gate_pattern(0, HALF, HALF)
        quantize_y(0, 0, HALF)
        quantize_y(0, HALF, HALF)
        gate_pattern(1, 0, HALF)
        round_w2(1, 1, nc.vector.tensor_copy, tag="gate1_0")
        quantize_y(1, 0, HALF)
        quantize_w2(1, 1)
        gate_pattern(1, HALF, HALF, tag="w2_raw11_0")
        quantize_y(1, HALF, HALF)

        act = {}
        f_bf = {}
        f_q = {}

        def columns(pieces, b, first, width):
            start = max(key[1] for key in pieces if key[0] == b and key[1] <= first)
            cols = slice(first - start, first - start + width)
            return pieces[b, start][0][:, cols].bitcast(FP8X4), pieces[b, start][1][:, cols]

        def hidden(b, first, width):
            act[b, first] = sb("act%d_%d" % (b, first), [P, PACK, width], F32, tag="h_sb%d%d" % (b, first // P))
            per_bank = BANK // width
            for t0 in range(0, PACK, per_bank):
                acc = bank([P, per_bank, width], "short" if HALF <= first < PICKS - P else "long")
                for u in range(per_bank):
                    cols = slice((t0 + u) * P, (t0 + u + 1) * P)
                    for a in two:
                        codes, scales = columns(y_q, a, first, width)
                        nc.tensor.matmul_mx(
                            out=acc[:, u, :],
                            lhsT=w2_q[a, b][0][:, cols].bitcast(FP8X4),
                            lhsT_scale=w2_q[a, b][1][:, cols],
                            rhs=codes,
                            rhs_scale=scales,
                            start=(a == 0),
                            stop=(a == 1),
                        )
                for u in range(per_bank):
                    t = t0 + u
                    nc.scalar.activation(
                        out=act[b, first][:, t, :], in_=acc[:, u, :], func=ACT.Gelu_apprx_tanh, bias=b2_sb[:, b, t : t + 1]
                    )

        def apply_gain(b, first, width, tag=""):
            f_bf[b, first] = sb("f_bf%d_%d" % (b, first), [P, width, PACK], BF16, tag=tag)
            nc.vector.tensor_tensor(
                f_bf[b, first][:].rearrange("p (c i) t -> p c t i", i=4),
                act[b, first][:].rearrange("p t (c i) -> p c t i", i=4),
                gain_sb[:, b, :].unsqueeze(1).unsqueeze(3).to_broadcast([P, width // 4, PACK, 4]),
                MULT,
            )

        def quantize_f(b, first, width):
            f_q[b, first] = quantize("f_%d_%d" % (b, first), f_bf[b, first], width)

        def features(first, width, n0, n1, copy=nc.scalar.copy):
            acc = bank([P, n1 - n0, width], "long")
            steps = [(w4_sb[:, a, :], w4_scale_sb[:, a, :], y_q, a) for a in two]
            steps += [(w3_q[a][0][:], w3_q[a][1][:], f_q, a) for a in two]
            for step, (words, planes, pieces, a) in enumerate(steps):
                codes, scales = columns(pieces, a, first, width)
                for n in range(n0, n1):
                    cols = slice(n * P, (n + 1) * P)
                    nc.tensor.matmul_mx(
                        out=acc[:, n - n0, :],
                        lhsT=words[:, cols].bitcast(FP8X4),
                        lhsT_scale=planes[:, cols],
                        rhs=codes,
                        rhs_scale=scales,
                        start=(step == 0 and n == n0),
                        stop=(step == len(steps) - 1 and n == n1 - 1),
                    )
            result = sb("result%d_%d" % (first, n0), [P, n1 - n0, width], F32)
            copy(result[:], acc[:])
            rows = out[n0 * P : n1 * P, first : first + width]
            nc.sync.dma_start(rows.rearrange("(n p) m -> p n m", p=P), result[:])

        pieces = [(0, 0, HALF), (1, 0, HALF), (0, HALF, HALF), (1, HALF, P), (1, HALF + P, P)]
        for piece in pieces:
            hidden(*piece)
        apply_gain(*pieces[0], tag="picked11")
        apply_gain(*pieces[1], tag="pat_sb1")
        quantize_f(*pieces[0])
        quantize_f(*pieces[1])
        apply_gain(*pieces[2])
        features(0, HALF, 0, 2)
        features(0, HALF, 2, 3)
        apply_gain(*pieces[3])
        quantize_f(*pieces[2])
        apply_gain(*pieces[4])
        quantize_f(*pieces[3])
        features(HALF, P, 0, 3)
        quantize_f(*pieces[4])
        features(HALF + P, P, 0, 3, copy=nc.vector.tensor_copy)
